import numpy as np
import ml_dtypes


def mxq(x, axis, fmt="e4m3"):
    dtype, down = {"e4m3": (ml_dtypes.float8_e4m3fn, 7), "e5m2": (ml_dtypes.float8_e5m2, 14)}[fmt]
    v = np.moveaxis(np.asarray(x, np.float32).astype(ml_dtypes.bfloat16).astype(np.float64), axis, -1)
    blocks = v.reshape(v.shape[:-1] + (-1, 32))
    amax = np.abs(blocks).max(-1, keepdims=True)
    byte = np.maximum(np.where(amax > 0, np.frexp(amax)[1] - 1 + 127, 0) - down, 1)
    scale = np.exp2(byte - 127.0)
    codes = (blocks / scale).astype(np.float32).astype(dtype).astype(np.float64)
    return np.moveaxis((codes * scale).reshape(v.shape), -1, axis)


WIDE = False


def mx_kscale(k):
    if not WIDE:
        return np.ones(k)
    levels = np.array([10, -10, 5, -5, 0])
    if k % 512:
        return np.exp2(np.random.permutation(np.resize(levels, k // 32))).repeat(32)
    a = np.empty((k // 512, 16))
    for p in range(k // 512):
        a[p, :8] = np.random.permutation(np.resize(levels, 8))
        for g in range(8):
            far = levels[np.abs(levels - a[p, g]) >= 10]
            a[p, g + 8] = far[np.random.randint(len(far))]
    return np.exp2(a.ravel()).repeat(32)


def f64(x):
    return np.asarray(x).astype(np.float64)


def striped8(idx):
    return np.asarray(idx).reshape(8, -1, 16).transpose(0, 2, 1).reshape(128, -1).astype(np.uint16)


def unstriped8(offs):
    return offs.reshape(8, 16, -1).transpose(0, 2, 1).reshape(8, -1).astype(np.int64)


def pick8(x, idx, run):
    r = np.arange(len(x))
    return x[r[:, None], idx[r % (8 * run) // run]]


E2M1 = np.array([0.0, 0.5, 1.0, 1.5, 2.0, 3.0, 4.0, 6.0, -0.0, -0.5, -1.0, -1.5, -2.0, -3.0, -4.0, -6.0])


def pack_weight(w, fmt):
    k, n = w.shape
    w = f64(np.asarray(w, np.float32).astype(ml_dtypes.bfloat16)).reshape(k // 32, 32, n)
    amax = np.abs(w).max(1)
    if fmt == "e4m3":
        byte = np.frexp(amax)[1] - 1 + 127 - 7
    else:
        mant, ex = np.frexp(amax / 6.0)
        byte = np.where(mant > 0.5, ex, ex - 1) + 127
    byte = np.clip(np.where(amax > 0, byte, 1), 1, 254)
    scaled = (w * np.exp2(127.0 - byte)[:, None, :]).reshape(k, n).astype(np.float32)
    by_word = np.ascontiguousarray(scaled.reshape(k // 512, 128, 4, n).transpose(0, 1, 3, 2))
    if fmt == "e4m3":
        words = by_word.astype(ml_dtypes.float8_e4m3fn).view(np.uint8)
    else:
        c = by_word.astype(ml_dtypes.float4_e2m1fn).view(np.uint8) & 0xF
        words = (c[..., 0::2] | (c[..., 1::2] << 4)).reshape(k // 512, 128, 2 * n)
    return np.ascontiguousarray(words), np.ascontiguousarray(byte.astype(np.uint8).reshape(k // 512, 16, n))


def unpack_weight(words, scales, fmt):
    g, _, n = scales.shape
    words = np.ascontiguousarray(words).reshape(g, 128, n, -1)
    if fmt == "e4m3":
        vals = words.view(ml_dtypes.float8_e4m3fn).astype(np.float64)
    else:
        nib = np.empty((g, 128, n, 4), np.uint8)
        nib[..., 0::2] = words & 0xF
        nib[..., 1::2] = words >> 4
        vals = E2M1[nib]
    vals = vals * np.repeat(np.exp2(scales.astype(np.float64) - 127.0), 8, axis=1)[..., None]
    return vals.transpose(0, 1, 3, 2).reshape(g * 512, n)


K, T, J, N, B = 512, 512, 1024, 512, 128


def setup_inputs():
    n = np.random.standard_normal
    idx = np.stack([np.random.randint(0, T, J) for _ in range(8)])
    fk = mx_kscale(K)
    xtp = pack_weight(n((K, T)) / fk[:, None], "e4m3")
    return {
        "xt_words": xtp[0],
        "xt_scales": xtp[1],
        "w": (n((K, N)) * 1 / np.sqrt(K) * fk[:, None]).astype(np.float32),
        "lam": (np.random.uniform(0.2, 0.9, (N, 1))).astype(np.float32),
        "offs": striped8(idx),
    }


def reference(xt_words, xt_scales, w, lam, offs):
    idx = unstriped8(offs)
    xtu = unpack_weight(xt_words, xt_scales, "e4m3")
    wq = mxq(f64(w), 0, "e4m3")
    z = wq.T @ xtu
    u = pick8(z, idx, 64)
    y = u.reshape(N, B, J // B).max(axis=2) - f64(lam) * u.reshape(N, B, J // B).mean(axis=2)
    return y

@@ -1,0 +1,174 @@
+from contextlib import ExitStack
+
+import concourse.mybir as mybir
+from concourse.masks import make_identity
+
+K, T, J, N, B = 512, 512, 1024, 512, 128
+FLOPS = 2 * K * N * T
+
+F32 = mybir.dt.float32
+BF16 = mybir.dt.bfloat16
+I32 = mybir.dt.int32
+U32 = mybir.dt.uint32
+U16 = mybir.dt.uint16
+U8 = mybir.dt.uint8
+FP8X4 = mybir.dt.float8_e4m3fn_x4
+ALU = mybir.AluOpType
+
+P = 128
+PACK = 4
+TILES = N // P
+GROUP = J // B
+HALF = J // 2
+WINDOW = 2 * T
+VECTOR_COLS = 88
+
+
+def tile_list_head_peaks_of_groups_kernel(tc, xt_words, xt_scales, w, lam, offs, out):
+    nc = tc.nc
+    with ExitStack() as ctx:
+        keep = ctx.enter_context(tc.tile_pool(name="keep", bufs=1))
+        psum = ctx.enter_context(tc.psum_pool(name="psum", bufs=1))
+        psum2 = ctx.enter_context(tc.psum_pool(name="psum2", bufs=2))
+
+        w_raw = keep.tile([P, PACK * N], F32, name="w_raw")
+        x_codes = keep.tile([P, T], U32, name="x_codes", align_bytes=64)
+        x_scales = keep.tile([P, T], U8, name="x_scales", align_bytes=64)
+        offsets = keep.tile([P, J // 16], U16, name="offsets")
+        lam_sb = keep.tile([P, TILES], F32, name="lam_sb")
+        share = keep.tile([P, TILES], F32, name="share")
+        ident = keep.tile([P, P], F32, name="ident")
+
+        nc.vector.memset(x_scales[:].bitcast(I32), 0)
+        nc.sync.dma_start(out=w_raw[:], in_=w.rearrange("(p j) n -> p (j n)", j=PACK))
+        nc.sync.dma_start(
+            out=x_codes[:].bitcast(I32),
+            in_=xt_words[0].rearrange("p c r -> p (c r)").bitcast(I32),
+        )
+        nc.sync.dma_start(offsets[:], offs)
+        nc.sync.dma_start(out=lam_sb[:], in_=lam.rearrange("(p q) o -> p (q o)", q=TILES))
+        for quad in range(4):
+            nc.scalar.dma_start(
+                out=x_scales[32 * quad : 32 * quad + 4, :].bitcast(I32),
+                in_=xt_scales[0, 4 * quad : 4 * quad + 4, :].bitcast(I32),
+            )
+        make_identity(nc, ident[:])
+
+        z = [keep.tile([P, WINDOW], F32, name="z%d" % q) for q in range(TILES)]
+        for q in range(TILES):
+            nc.vector.memset(z[q][:, T:], 0.0)
+        nc.vector.tensor_scalar(
+            out=share[:], in0=lam_sb[:], scalar1=-1.0 / GROUP, scalar2=None, op0=ALU.mult
+        )
+
+        w_bf = [keep.tile([P, P * PACK], BF16, name="w_bf%d" % q, align_bytes=64) for q in range(TILES)]
+        w_codes = [keep.tile([P, P], U32, name="w_codes%d" % q, align_bytes=64) for q in range(TILES)]
+        w_scales = [keep.tile([P, P], U8, name="w_scales%d" % q, align_bytes=64) for q in range(TILES)]
+        w_view = w_raw[:].rearrange("p (j m q) -> p q m j", j=PACK, q=TILES)
+
+        def cast(copy, q, m0, m1):
+            dst = w_bf[q][:].rearrange("p (m j) -> p m j", j=PACK)
+            copy(out=dst[:, m0:m1, :], in_=w_view[:, q, m0:m1, :])
+
+        def quantise(q):
+            nc.vector.quantize_mx(out=w_codes[q][:].bitcast(FP8X4), scales=w_scales[q][:], in_=w_bf[q][:])
+
+        def product(q, acc, t0, t1):
+            nc.tensor.matmul_mx(
+                out=acc,
+                lhsT=w_codes[q][:].bitcast(FP8X4),
+                lhsT_scale=w_scales[q][:],
+                rhs=x_codes[:, t0:t1].bitcast(FP8X4),
+                rhs_scale=x_scales[:, t0:t1],
+                start=True,
+                stop=True,
+            )
+
+        cast(nc.vector.tensor_copy, 0, 0, VECTOR_COLS)
+        cast(nc.scalar.copy, 0, VECTOR_COLS, P)
+        quantise(0)
+        first_lo = psum.tile([P, T // 2], F32, name="first_lo")
+        first_hi = psum.tile([P, T // 2], F32, name="first_hi")
+        product(0, first_lo[:], 0, T // 2)
+        product(0, first_hi[:], T // 2, T)
+        cast(nc.scalar.copy, 1, 0, P)
+        cast(nc.vector.tensor_copy, 2, 0, P)
+        quantise(1)
+        nc.scalar.copy(out=z[0][:, 0 : T // 2], in_=first_lo[:])
+        nc.vector.tensor_copy(out=z[0][:, T // 2 : T], in_=first_hi[:])
+        quantise(2)
+        cast(nc.scalar.copy, 3, 0, P)
+
+        u = keep.tile([P, TILES * J], F32, name="u")
+        sums = []
+
+        def gather(q):
+            for h in range(2):
+                nc.vector.tensor_copy(
+                    out=u[:, q * J + h * HALF : q * J + (h + 1) * HALF],
+                    in_=z[q][:].indirect(offsets[:, h * (HALF // 16) : (h + 1) * (HALF // 16)]),
+                )
+
+        def features(q):
+            acc = psum2.tile([P, T], F32, name="acc")
+            product(q, acc[:], 0, T)
+            nc.scalar.copy(out=z[q][:, 0:T], in_=acc[:])
+
+        def group_sums(q):
+            turned = psum2.tile([P, P], F32, name="turned")
+            for i in range(GROUP):
+                nc.tensor.matmul(
+                    turned[:],
+                    lhsT=u[:, q * J + i : (q + 1) * J : GROUP],
+                    rhs=ident[:],
+                    start=(i == 0),
+                    stop=(i == GROUP - 1),
+                    is_transpose=True,
+                )
+            turned_sb = keep.tile([P, P], F32, name="turned_sb%d" % q)
+            nc.scalar.copy(out=turned_sb[:], in_=turned[:])
+            nc.tensor.transpose(sum_bank[q // 2][:, (q % 2) * B : (q % 2 + 1) * B], turned_sb[:], ident[:])
+
+        sum_bank = [psum2.tile([P, 2 * B], F32, name="sum_bank") for pair in range(2)]
+
+        features(1)
+        gather(0)
+        quantise(3)
+        features(2)
+        features(3)
+        group_sums(0)
+        for q in range(1, TILES):
+            gather(q)
+            group_sums(q)
+
+        m4 = keep.tile([P, TILES * J // 2], F32, name="m4")
+        m2 = keep.tile([P, TILES * J // 4], F32, name="m2")
+        m1 = keep.tile([P, TILES * B], F32, name="m1")
+        res = keep.tile([P, TILES * B], F32, name="res")
+
+        def halve(dst, src, width, g0, g1):
+            pairs = src[:, g0 * width : g1 * width].rearrange("p (g h e) -> p g h e", h=2, e=width // 2)
+            kept = dst[:, g0 * width // 2 : g1 * width // 2].rearrange("p (g e) -> p g e", e=width // 2)
+            nc.vector.tensor_tensor(out=kept, in0=pairs[:, :, 0, :], in1=pairs[:, :, 1, :], op=ALU.max)
+
+        groups = TILES * B
+        halve(m4, u, 8, 0, groups - B // 2)
+        halve(m4, u, 8, groups - B // 2, groups)
+        for dst, src, width in ((m2, m4, 4), (m1, m2, 2)):
+            halve(dst, src, width, 0, groups // 2)
+            halve(dst, src, width, groups // 2, groups)
+
+        out_rows = out.rearrange("(p q) b -> p (q b)", q=TILES)
+        for q in range(TILES):
+            cols = slice(q * B, (q + 1) * B)
+            nc.vector.scalar_tensor_tensor(
+                out=res[:, cols],
+                in0=sum_bank[q // 2][:, (q % 2) * B : (q % 2 + 1) * B],
+                scalar=share[:, q : q + 1],
+                in1=m1[:, cols],
+                op0=ALU.mult,
+                op1=ALU.add,
+            )
+            if q % 2 == 1:
+                pair = slice((q - 1) * B, (q + 1) * B)
+                nc.sync.dma_start(out=out_rows[:, pair], in_=res[:, pair])

@@ -36,7 +36,6 @@ def tile_list_head_peaks_of_groups_kernel(tc, xt_words, xt_scales, w, lam, offs,
         x_scales = keep.tile([P, T], U8, name="x_scales", align_bytes=64)
         offsets = keep.tile([P, J // 16], U16, name="offsets")
         lam_sb = keep.tile([P, TILES], F32, name="lam_sb")
-        share = keep.tile([P, TILES], F32, name="share")
         ident = keep.tile([P, P], F32, name="ident")
 
         nc.vector.memset(x_scales[:].bitcast(I32), 0)
@@ -54,59 +53,62 @@ def tile_list_head_peaks_of_groups_kernel(tc, xt_words, xt_scales, w, lam, offs,
             )
         make_identity(nc, ident[:])
 
-        z = [keep.tile([P, WINDOW], F32, name="z%d" % q) for q in range(TILES)]
-        for q in range(TILES):
-            nc.vector.memset(z[q][:, T:], 0.0)
-        nc.vector.tensor_scalar(
-            out=share[:], in0=lam_sb[:], scalar1=-1.0 / GROUP, scalar2=None, op0=ALU.mult
-        )
+        pieces = [1, 1, 1, 2]
+        z = [keep.tile([P, 2 * J // pieces[q]], F32, name="z%d" % q) for q in range(TILES)]
 
-        w_bf = [keep.tile([P, P * PACK], BF16, name="w_bf%d" % q, align_bytes=64) for q in range(TILES)]
-        w_codes = [keep.tile([P, P], U32, name="w_codes%d" % q, align_bytes=64) for q in range(TILES)]
-        w_scales = [keep.tile([P, P], U8, name="w_scales%d" % q, align_bytes=64) for q in range(TILES)]
-        w_view = w_raw[:].rearrange("p (j m q) -> p q m j", j=PACK, q=TILES)
+        stage = keep.tile([P, 3 * P * PACK], BF16, name="stage", align_bytes=64)
+        w_codes = keep.tile([P, N], U32, name="w_codes", align_bytes=64)
+        w_scales = keep.tile([P, N], U8, name="w_scales", align_bytes=64)
+        w_view = w_raw[:].rearrange("p (j m q) -> p m j q", j=PACK, q=TILES)
+        width = P * PACK
+        place = [width, 2 * width, 0, width]
 
-        def cast(copy, q, m0, m1):
-            dst = w_bf[q][:].rearrange("p (m j) -> p m j", j=PACK)
-            copy(out=dst[:, m0:m1, :], in_=w_view[:, q, m0:m1, :])
+        def cast_pair(q, split):
+            dst = stage[:, place[q] : place[q] + 2 * width].rearrange("p (q m j) -> p m j q", q=2, j=PACK)
+            for copy, m0, m1 in ((nc.vector.tensor_copy, 0, split), (nc.scalar.copy, split, P)):
+                if m1 > m0:
+                    copy(out=dst[:, m0:m1], in_=w_view[:, m0:m1, :, q : q + 2])
 
-        def quantise(q):
-            nc.vector.quantize_mx(out=w_codes[q][:].bitcast(FP8X4), scales=w_scales[q][:], in_=w_bf[q][:])
+        def quantise(q, count):
+            cols = slice(q * P, (q + count) * P)
+            nc.vector.quantize_mx(
+                out=w_codes[:, cols].bitcast(FP8X4),
+                scales=w_scales[:, cols],
+                in_=stage[:, place[q] : place[q] + count * width],
+            )
 
         def product(q, acc, t0, t1):
             nc.tensor.matmul_mx(
                 out=acc,
-                lhsT=w_codes[q][:].bitcast(FP8X4),
-                lhsT_scale=w_scales[q][:],
+                lhsT=w_codes[:, q * P : (q + 1) * P].bitcast(FP8X4),
+                lhsT_scale=w_scales[:, q * P : (q + 1) * P],
                 rhs=x_codes[:, t0:t1].bitcast(FP8X4),
                 rhs_scale=x_scales[:, t0:t1],
                 start=True,
                 stop=True,
             )
 
-        cast(nc.vector.tensor_copy, 0, 0, VECTOR_COLS)
-        cast(nc.scalar.copy, 0, VECTOR_COLS, P)
-        quantise(0)
+        cast_pair(0, VECTOR_COLS)
+        quantise(0, 1)
+        quantise(1, 1)
         first_lo = psum.tile([P, T // 2], F32, name="first_lo")
         first_hi = psum.tile([P, T // 2], F32, name="first_hi")
         product(0, first_lo[:], 0, T // 2)
         product(0, first_hi[:], T // 2, T)
-        cast(nc.scalar.copy, 1, 0, P)
-        cast(nc.vector.tensor_copy, 2, 0, P)
-        quantise(1)
+        cast_pair(2, P)
+        quantise(2, 2)
         nc.scalar.copy(out=z[0][:, 0 : T // 2], in_=first_lo[:])
-        nc.vector.tensor_copy(out=z[0][:, T // 2 : T], in_=first_hi[:])
-        quantise(2)
-        cast(nc.scalar.copy, 3, 0, P)
+        nc.scalar.copy(out=z[0][:, T // 2 : T], in_=first_hi[:])
 
         u = keep.tile([P, TILES * J], F32, name="u")
         sums = []
 
         def gather(q):
-            for h in range(2):
+            size = J // pieces[q]
+            for h in range(pieces[q]):
                 nc.vector.tensor_copy(
-                    out=u[:, q * J + h * HALF : q * J + (h + 1) * HALF],
-                    in_=z[q][:].indirect(offsets[:, h * (HALF // 16) : (h + 1) * (HALF // 16)]),
+                    out=u[:, q * J + h * size : q * J + (h + 1) * size],
+                    in_=z[q][:].indirect(offsets[:, h * (size // 16) : (h + 1) * (size // 16)]),
                 )
 
         def features(q):
@@ -126,14 +128,13 @@ def tile_list_head_peaks_of_groups_kernel(tc, xt_words, xt_scales, w, lam, offs,
                     is_transpose=True,
                 )
             turned_sb = keep.tile([P, P], F32, name="turned_sb%d" % q)
-            nc.scalar.copy(out=turned_sb[:], in_=turned[:])
+            nc.scalar.activation(out=turned_sb[:], in_=turned[:], func=mybir.ActivationFunctionType.Copy, scale=-1.0 / GROUP)
             nc.tensor.transpose(sum_bank[q // 2][:, (q % 2) * B : (q % 2 + 1) * B], turned_sb[:], ident[:])
 
         sum_bank = [psum2.tile([P, 2 * B], F32, name="sum_bank") for pair in range(2)]
 
         features(1)
         gather(0)
-        quantise(3)
         features(2)
         features(3)
         group_sums(0)
@@ -164,11 +165,11 @@ def tile_list_head_peaks_of_groups_kernel(tc, xt_words, xt_scales, w, lam, offs,
             nc.vector.scalar_tensor_tensor(
                 out=res[:, cols],
                 in0=sum_bank[q // 2][:, (q % 2) * B : (q % 2 + 1) * B],
-                scalar=share[:, q : q + 1],
+                scalar=lam_sb[:, q : q + 1],
                 in1=m1[:, cols],
                 op0=ALU.mult,
                 op1=ALU.add,
             )
-            if q % 2 == 1:
-                pair = slice((q - 1) * B, (q + 1) * B)
-                nc.sync.dma_start(out=out_rows[:, pair], in_=res[:, pair])
+            if q >= 1:
+                done = slice(0 if q == 1 else q * B, (q + 1) * B)
+                nc.sync.dma_start(out=out_rows[:, done], in_=res[:, done])

@@ -14,6 +14,7 @@ U16 = mybir.dt.uint16
 U8 = mybir.dt.uint8
 FP8X4 = mybir.dt.float8_e4m3fn_x4
 ALU = mybir.AluOpType
+ACT = mybir.ActivationFunctionType
 
 P = 128
 PACK = 4
@@ -127,22 +128,46 @@ def tile_list_head_peaks_of_groups_kernel(tc, xt_words, xt_scales, w, lam, offs,
                     stop=(i == GROUP - 1),
                     is_transpose=True,
                 )
-            turned_sb = keep.tile([P, P], F32, name="turned_sb%d" % q)
-            nc.scalar.activation(out=turned_sb[:], in_=turned[:], func=mybir.ActivationFunctionType.Copy, scale=-1.0 / GROUP)
-            nc.tensor.transpose(sum_bank[q // 2][:, (q % 2) * B : (q % 2 + 1) * B], turned_sb[:], ident[:])
+            turned_sb = gap[min(q, 1)][:, q * P : (q + 1) * P]
+            nc.scalar.activation(out=turned_sb, in_=turned[:], func=ACT.Copy, scale=-1.0 / GROUP)
+            bank = psum.tile([P, B], F32, name=("sum0", "sum1", "first_lo", "first_hi")[q])
+            nc.tensor.transpose(bank[:], turned_sb, ident[:])
+            sums.append(bank)
 
-        sum_bank = [psum2.tile([P, 2 * B], F32, name="sum_bank") for pair in range(2)]
+        m4 = keep.tile([P, TILES * J // 2], F32, name="m4")
+        gap = [keep.tile([P, HALF], F32, name="gap%d" % q) for q in range(2)]
+        rise = [keep.tile([P, HALF], F32, name="rise%d" % q) for q in range(2)]
+
+        def halve_aside(q):
+            pairs = u[:, q * J : (q + 1) * J].rearrange("p (g h e) -> p g h e", h=2, e=GROUP // 2)
+            shape = "p (g e) -> p g e"
+            nc.gpsimd.tensor_tensor(
+                out=gap[q][:].rearrange(shape, e=GROUP // 2),
+                in0=pairs[:, :, 0, :],
+                in1=pairs[:, :, 1, :],
+                op=ALU.subtract,
+            )
+            nc.scalar.activation(out=rise[q][:], in_=gap[q][:], func=ACT.Relu)
+            nc.gpsimd.tensor_tensor(
+                out=m4[:, q * HALF : (q + 1) * HALF].rearrange(shape, e=GROUP // 2),
+                in0=rise[q][:].rearrange(shape, e=GROUP // 2),
+                in1=pairs[:, :, 1, :],
+                op=ALU.add,
+            )
 
         features(1)
         gather(0)
         features(2)
         features(3)
+        halve_aside(0)
         group_sums(0)
-        for q in range(1, TILES):
+        gather(1)
+        halve_aside(1)
+        group_sums(1)
+        for q in range(2, TILES):
             gather(q)
             group_sums(q)
 
-        m4 = keep.tile([P, TILES * J // 2], F32, name="m4")
         m2 = keep.tile([P, TILES * J // 4], F32, name="m2")
         m1 = keep.tile([P, TILES * B], F32, name="m1")
         res = keep.tile([P, TILES * B], F32, name="res")
@@ -153,18 +178,18 @@ def tile_list_head_peaks_of_groups_kernel(tc, xt_words, xt_scales, w, lam, offs,
             nc.vector.tensor_tensor(out=kept, in0=pairs[:, :, 0, :], in1=pairs[:, :, 1, :], op=ALU.max)
 
         groups = TILES * B
-        halve(m4, u, 8, 0, groups - B // 2)
+        halve(m4, u, 8, 2 * B, groups - B // 2)
         halve(m4, u, 8, groups - B // 2, groups)
         for dst, src, width in ((m2, m4, 4), (m1, m2, 2)):
-            halve(dst, src, width, 0, groups // 2)
-            halve(dst, src, width, groups // 2, groups)
+            halve(dst, src, width, 0, 3 * B // 2)
+            halve(dst, src, width, 3 * B // 2, groups)
 
         out_rows = out.rearrange("(p q) b -> p (q b)", q=TILES)
         for q in range(TILES):
             cols = slice(q * B, (q + 1) * B)
             nc.vector.scalar_tensor_tensor(
                 out=res[:, cols],
-                in0=sum_bank[q // 2][:, (q % 2) * B : (q % 2 + 1) * B],
+                in0=sums[q][:],
                 scalar=lam_sb[:, q : q + 1],
                 in1=m1[:, cols],
                 op0=ALU.mult,

@@ -54,8 +54,7 @@ def tile_list_head_peaks_of_groups_kernel(tc, xt_words, xt_scales, w, lam, offs,
             )
         make_identity(nc, ident[:])
 
-        pieces = [1, 1, 1, 2]
-        z = [keep.tile([P, 2 * J // pieces[q]], F32, name="z%d" % q) for q in range(TILES)]
+        z = [keep.tile([P, 2 * J], F32, name="z%d" % q) for q in range(TILES)]
 
         stage = keep.tile([P, 3 * P * PACK], BF16, name="stage", align_bytes=64)
         w_codes = keep.tile([P, N], U32, name="w_codes", align_bytes=64)
@@ -105,12 +104,7 @@ def tile_list_head_peaks_of_groups_kernel(tc, xt_words, xt_scales, w, lam, offs,
         sums = []
 
         def gather(q):
-            size = J // pieces[q]
-            for h in range(pieces[q]):
-                nc.vector.tensor_copy(
-                    out=u[:, q * J + h * size : q * J + (h + 1) * size],
-                    in_=z[q][:].indirect(offsets[:, h * (size // 16) : (h + 1) * (size // 16)]),
-                )
+            nc.vector.tensor_copy(out=u[:, q * J : (q + 1) * J], in_=z[q][:].indirect(offsets[:]))
 
         def features(q):
             acc = psum2.tile([P, T], F32, name="acc")
@@ -134,7 +128,7 @@ def tile_list_head_peaks_of_groups_kernel(tc, xt_words, xt_scales, w, lam, offs,
             nc.tensor.transpose(bank[:], turned_sb, ident[:])
             sums.append(bank)
 
-        m4 = keep.tile([P, TILES * J // 2], F32, name="m4")
+        m4 = keep.tile([P, J], F32, name="m4")
         gap = [keep.tile([P, HALF], F32, name="gap%d" % q) for q in range(2)]
         rise = [keep.tile([P, HALF], F32, name="rise%d" % q) for q in range(2)]
 
@@ -168,33 +162,52 @@ def tile_list_head_peaks_of_groups_kernel(tc, xt_words, xt_scales, w, lam, offs,
             gather(q)
             group_sums(q)
 
-        m2 = keep.tile([P, TILES * J // 4], F32, name="m2")
-        m1 = keep.tile([P, TILES * B], F32, name="m1")
+        m2 = keep.tile([P, HALF], F32, name="m2")
+        m1 = keep.tile([P, 2 * B], F32, name="m1")
+        m2_late = keep.tile([P, 2 * B], F32, name="m2_late")
+        m1_late = keep.tile([P, B], F32, name="m1_late")
+        share = keep.tile([P, 2 * B], F32, name="share")
         res = keep.tile([P, TILES * B], F32, name="res")
+        for q in range(2):
+            nc.scalar.activation(
+                out=share[:, q * B : (q + 1) * B], in_=sums[q][:], func=ACT.Copy, scale=lam_sb[:, q : q + 1]
+            )
 
-        def halve(dst, src, width, g0, g1):
-            pairs = src[:, g0 * width : g1 * width].rearrange("p (g h e) -> p g h e", h=2, e=width // 2)
-            kept = dst[:, g0 * width // 2 : g1 * width // 2].rearrange("p (g e) -> p g e", e=width // 2)
+        def halve(dst, src, width):
+            pairs = src.rearrange("p (g h e) -> p g h e", h=2, e=width // 2)
+            kept = dst.rearrange("p (g e) -> p g e", e=width // 2)
             nc.vector.tensor_tensor(out=kept, in0=pairs[:, :, 0, :], in1=pairs[:, :, 1, :], op=ALU.max)
 
-        groups = TILES * B
-        halve(m4, u, 8, 2 * B, groups - B // 2)
-        halve(m4, u, 8, groups - B // 2, groups)
-        for dst, src, width in ((m2, m4, 4), (m1, m2, 2)):
-            halve(dst, src, width, 0, 3 * B // 2)
-            halve(dst, src, width, 3 * B // 2, groups)
-
         out_rows = out.rearrange("(p q) b -> p (q b)", q=TILES)
-        for q in range(TILES):
+
+        def finish(q, top):
             cols = slice(q * B, (q + 1) * B)
             nc.vector.scalar_tensor_tensor(
                 out=res[:, cols],
                 in0=sums[q][:],
                 scalar=lam_sb[:, q : q + 1],
-                in1=m1[:, cols],
+                in1=top,
                 op0=ALU.mult,
                 op1=ALU.add,
             )
-            if q >= 1:
-                done = slice(0 if q == 1 else q * B, (q + 1) * B)
-                nc.sync.dma_start(out=out_rows[:, done], in_=res[:, done])
+            nc.sync.dma_start(out=out_rows[:, cols], in_=res[:, cols])
+
+        def peaks(h):
+            nc.vector.tensor_reduce(
+                out=m2[:, h * B // 2 : (h + 1) * B // 2],
+                in_=u[:, 3 * J + h * HALF : 3 * J + (h + 1) * HALF].rearrange("p (g i) -> p g i", i=GROUP),
+                axis=mybir.AxisListType.X,
+                op=ALU.max,
+            )
+
+        halve(m2[:], m4[:], 4)
+        halve(rise[1][:], u[:, 2 * J : 3 * J], 8)
+        halve(m1[:], m2[:], 2)
+        nc.gpsimd.tensor_tensor(out=res[:, 0 : 2 * B], in0=m1[:], in1=share[:], op=ALU.add)
+        nc.sync.dma_start(out=out_rows[:, 0 : 2 * B], in_=res[:, 0 : 2 * B])
+        halve(m2_late[:], rise[1][:], 4)
+        peaks(0)
+        halve(m1_late[:], m2_late[:], 2)
+        peaks(1)
+        finish(2, m1_late[:])
+        finish(3, m2[:, 0:B])

from contextlib import ExitStack

import concourse.mybir as mybir
from concourse.masks import make_identity

K, T, J, N, B = 512, 512, 1024, 512, 128
FLOPS = 2 * K * N * T

F32 = mybir.dt.float32
BF16 = mybir.dt.bfloat16
I32 = mybir.dt.int32
U32 = mybir.dt.uint32
U16 = mybir.dt.uint16
U8 = mybir.dt.uint8
FP8X4 = mybir.dt.float8_e4m3fn_x4
ALU = mybir.AluOpType
ACT = mybir.ActivationFunctionType

P = 128
PACK = 4
TILES = N // P
GROUP = J // B
HALF = J // 2
WINDOW = 2 * T
VECTOR_COLS = 88


def tile_list_head_peaks_of_groups_kernel(tc, xt_words, xt_scales, w, lam, offs, out):
    nc = tc.nc
    with ExitStack() as ctx:
        keep = ctx.enter_context(tc.tile_pool(name="keep", bufs=1))
        psum = ctx.enter_context(tc.psum_pool(name="psum", bufs=1))
        psum2 = ctx.enter_context(tc.psum_pool(name="psum2", bufs=2))

        w_raw = keep.tile([P, PACK * N], F32, name="w_raw")
        x_codes = keep.tile([P, T], U32, name="x_codes", align_bytes=64)
        x_scales = keep.tile([P, T], U8, name="x_scales", align_bytes=64)
        offsets = keep.tile([P, J // 16], U16, name="offsets")
        lam_sb = keep.tile([P, TILES], F32, name="lam_sb")
        ident = keep.tile([P, P], F32, name="ident")

        nc.vector.memset(x_scales[:].bitcast(I32), 0)
        nc.sync.dma_start(out=w_raw[:], in_=w.rearrange("(p j) n -> p (j n)", j=PACK))
        nc.sync.dma_start(
            out=x_codes[:].bitcast(I32),
            in_=xt_words[0].rearrange("p c r -> p (c r)").bitcast(I32),
        )
        nc.sync.dma_start(offsets[:], offs)
        nc.sync.dma_start(out=lam_sb[:], in_=lam.rearrange("(p q) o -> p (q o)", q=TILES))
        for quad in range(4):
            nc.scalar.dma_start(
                out=x_scales[32 * quad : 32 * quad + 4, :].bitcast(I32),
                in_=xt_scales[0, 4 * quad : 4 * quad + 4, :].bitcast(I32),
            )
        make_identity(nc, ident[:])

        z = [keep.tile([P, 2 * J], F32, name="z%d" % q) for q in range(TILES)]

        stage = keep.tile([P, 3 * P * PACK], BF16, name="stage", align_bytes=64)
        w_codes = keep.tile([P, N], U32, name="w_codes", align_bytes=64)
        w_scales = keep.tile([P, N], U8, name="w_scales", align_bytes=64)
        w_view = w_raw[:].rearrange("p (j m q) -> p m j q", j=PACK, q=TILES)
        width = P * PACK
        place = [width, 2 * width, 0, width]

        def cast_pair(q, split):
            dst = stage[:, place[q] : place[q] + 2 * width].rearrange("p (q m j) -> p m j q", q=2, j=PACK)
            for copy, m0, m1 in ((nc.vector.tensor_copy, 0, split), (nc.scalar.copy, split, P)):
                if m1 > m0:
                    copy(out=dst[:, m0:m1], in_=w_view[:, m0:m1, :, q : q + 2])

        def quantise(q, count):
            cols = slice(q * P, (q + count) * P)
            nc.vector.quantize_mx(
                out=w_codes[:, cols].bitcast(FP8X4),
                scales=w_scales[:, cols],
                in_=stage[:, place[q] : place[q] + count * width],
            )

        def product(q, acc, t0, t1):
            nc.tensor.matmul_mx(
                out=acc,
                lhsT=w_codes[:, q * P : (q + 1) * P].bitcast(FP8X4),
                lhsT_scale=w_scales[:, q * P : (q + 1) * P],
                rhs=x_codes[:, t0:t1].bitcast(FP8X4),
                rhs_scale=x_scales[:, t0:t1],
                start=True,
                stop=True,
            )

        cast_pair(0, VECTOR_COLS)
        quantise(0, 1)
        quantise(1, 1)
        first_lo = psum.tile([P, T // 2], F32, name="first_lo")
        first_hi = psum.tile([P, T // 2], F32, name="first_hi")
        product(0, first_lo[:], 0, T // 2)
        product(0, first_hi[:], T // 2, T)
        cast_pair(2, P)
        quantise(2, 2)
        nc.scalar.copy(out=z[0][:, 0 : T // 2], in_=first_lo[:])
        nc.scalar.copy(out=z[0][:, T // 2 : T], in_=first_hi[:])

        u = keep.tile([P, TILES * J], F32, name="u")
        sums = []

        def gather(q):
            nc.vector.tensor_copy(out=u[:, q * J : (q + 1) * J], in_=z[q][:].indirect(offsets[:]))

        def features(q):
            acc = psum2.tile([P, T], F32, name="acc")
            product(q, acc[:], 0, T)
            nc.scalar.copy(out=z[q][:, 0:T], in_=acc[:])

        def group_sums(q):
            turned = psum2.tile([P, P], F32, name="turned")
            for i in range(GROUP):
                nc.tensor.matmul(
                    turned[:],
                    lhsT=u[:, q * J + i : (q + 1) * J : GROUP],
                    rhs=ident[:],
                    start=(i == 0),
                    stop=(i == GROUP - 1),
                    is_transpose=True,
                )
            turned_sb = gap[min(q, 1)][:, q * P : (q + 1) * P]
            nc.scalar.activation(out=turned_sb, in_=turned[:], func=ACT.Copy, scale=-1.0 / GROUP)
            bank = psum.tile([P, B], F32, name=("sum0", "sum1", "first_lo", "first_hi")[q])
            nc.tensor.transpose(bank[:], turned_sb, ident[:])
            sums.append(bank)

        m4 = keep.tile([P, J], F32, name="m4")
        gap = [keep.tile([P, HALF], F32, name="gap%d" % q) for q in range(2)]
        rise = [keep.tile([P, HALF], F32, name="rise%d" % q) for q in range(2)]

        def halve_aside(q):
            pairs = u[:, q * J : (q + 1) * J].rearrange("p (g h e) -> p g h e", h=2, e=GROUP // 2)
            shape = "p (g e) -> p g e"
            nc.gpsimd.tensor_tensor(
                out=gap[q][:].rearrange(shape, e=GROUP // 2),
                in0=pairs[:, :, 0, :],
                in1=pairs[:, :, 1, :],
                op=ALU.subtract,
            )
            nc.scalar.activation(out=rise[q][:], in_=gap[q][:], func=ACT.Relu)
            nc.gpsimd.tensor_tensor(
                out=m4[:, q * HALF : (q + 1) * HALF].rearrange(shape, e=GROUP // 2),
                in0=rise[q][:].rearrange(shape, e=GROUP // 2),
                in1=pairs[:, :, 1, :],
                op=ALU.add,
            )

        features(1)
        gather(0)
        features(2)
        features(3)
        halve_aside(0)
        group_sums(0)
        gather(1)
        halve_aside(1)
        group_sums(1)
        for q in range(2, TILES):
            gather(q)
            group_sums(q)

        m2 = keep.tile([P, HALF], F32, name="m2")
        m1 = keep.tile([P, 2 * B], F32, name="m1")
        m2_late = keep.tile([P, 2 * B], F32, name="m2_late")
        m1_late = keep.tile([P, B], F32, name="m1_late")
        share = keep.tile([P, 2 * B], F32, name="share")
        res = keep.tile([P, TILES * B], F32, name="res")
        for q in range(2):
            nc.scalar.activation(
                out=share[:, q * B : (q + 1) * B], in_=sums[q][:], func=ACT.Copy, scale=lam_sb[:, q : q + 1]
            )

        def halve(dst, src, width):
            pairs = src.rearrange("p (g h e) -> p g h e", h=2, e=width // 2)
            kept = dst.rearrange("p (g e) -> p g e", e=width // 2)
            nc.vector.tensor_tensor(out=kept, in0=pairs[:, :, 0, :], in1=pairs[:, :, 1, :], op=ALU.max)

        out_rows = out.rearrange("(p q) b -> p (q b)", q=TILES)

        def finish(q, top):
            cols = slice(q * B, (q + 1) * B)
            nc.vector.scalar_tensor_tensor(
                out=res[:, cols],
                in0=sums[q][:],
                scalar=lam_sb[:, q : q + 1],
                in1=top,
                op0=ALU.mult,
                op1=ALU.add,
            )
            nc.sync.dma_start(out=out_rows[:, cols], in_=res[:, cols])

        def peaks(h):
            nc.vector.tensor_reduce(
                out=m2[:, h * B // 2 : (h + 1) * B // 2],
                in_=u[:, 3 * J + h * HALF : 3 * J + (h + 1) * HALF].rearrange("p (g i) -> p g i", i=GROUP),
                axis=mybir.AxisListType.X,
                op=ALU.max,
            )

        halve(m2[:], m4[:], 4)
        halve(rise[1][:], u[:, 2 * J : 3 * J], 8)
        halve(m1[:], m2[:], 2)
        nc.gpsimd.tensor_tensor(out=res[:, 0 : 2 * B], in0=m1[:], in1=share[:], op=ALU.add)
        nc.sync.dma_start(out=out_rows[:, 0 : 2 * B], in_=res[:, 0 : 2 * B])
        halve(m2_late[:], rise[1][:], 4)
        peaks(0)
        halve(m1_late[:], m2_late[:], 2)
        peaks(1)
        finish(2, m1_late[:])
        finish(3, m2[:, 0:B])
